import numpy as np, ml_dtypes
CORES = [2,3,10,11,18,19,26,27,34,35,42,43,50,51,58,59]
N = 16
def setup_inputs(rng):
    return {"x": rng.standard_normal((N, 128, 16), dtype=np.float32).astype(ml_dtypes.bfloat16)}
def reference(x):
    b = 16 // N
    blocks = x.reshape(N, 128, N, b)
    return {"y": np.ascontiguousarray(blocks.transpose(2, 1, 0, 3)).reshape(N, 128, 16)}

@@ -1,0 +1,38 @@
+from concourse.bass import DstId, RemoteDMATransfer
+
+SCRATCH = {
+    "xs": ("sbuf", [128, 16], "bfloat16"),
+    "land": ("sbuf", [128, 16], "bfloat16"),
+}
+SEMAPHORES = ["loaded", "arrived", "stored"]
+
+
+def rank_program(g, core, T, topo):
+    r = T.rank_of(core)
+    if r is None:
+        return
+    n = len(T.cores)
+
+    g.sync.dma_start(T.xs[:], T.x[:]).then_inc(T.sem.loaded, 16)
+
+    g.sync.wait_ge(T.sem.loaded, 16)
+    g.sync.dma_start(T.land[:, r:r + 1], T.xs[:, r:r + 1]).then_inc(T.sem.arrived, 16)
+
+    g.wait_ge(T.sem.loaded, 16)
+    off = [j for j in range(n) if topo.chip(T.cores[j]) != topo.chip(core)]
+    on = [j for j in range(n) if j != r and topo.chip(T.cores[j]) == topo.chip(core)]
+
+    def transfer(j, engine):
+        rid, pid, _se = topo.addr(T.cores[j])
+        return RemoteDMATransfer(dst_ids=[DstId(rid=rid, pnc=pid)], dma_engine_mask=1 << engine,
+                                 remote_sem=T.sem.arrived, src=T.xs[:, j:j + 1], dst=T.land[:, r:r + 1])
+
+    half = len(off) // 2
+    first = [transfer(j, e) for e, j in enumerate(off[:half])] + [transfer(j, 8 + e) for e, j in enumerate(on)]
+    second = [transfer(j, e) for e, j in enumerate(off[half:])]
+    g.remote_dma_fused(first, local_sem=T.sem.arrived)
+    g.remote_dma_fused(second, local_sem=T.sem.arrived)
+
+    g.wait_ge(T.sem.arrived, 16 + 2 * (n - 1))
+    g.dma_start(T.y[:], T.land[:]).then_inc(T.sem.stored, 16)
+    g.wait_ge(T.sem.stored, 16)

@@ -1,38 +1,89 @@
 from concourse.bass import DstId, RemoteDMATransfer
 
+HALF = 8
+
 SCRATCH = {
     "xs": ("sbuf", [128, 16], "bfloat16"),
+    "half": ("sbuf", [128, HALF], "bfloat16"),
     "land": ("sbuf", [128, 16], "bfloat16"),
 }
 SEMAPHORES = ["loaded", "arrived", "stored"]
 
+ROLES = {
+    2: {2: (1, 3), 0: (0, 2), 4: (4, 6), 6: (5, 7)},
+    3: {3: (5, 7), 1: (4, 6), 5: (0, 2), 7: (1, 3)},
+}
+FEED_ENGINES = 8
+
+
+def column_writes(sender, cores, topo):
+    chip, local = topo.chip(sender), sender % 8
+    owner = [c for c in cores if topo.chip(c) == chip and local in ROLES[c % 8]][0]
+    ds = ROLES[owner % 8][local]
+    dests = [j for j, c in enumerate(cores) if (topo.chip(c) ^ chip) in ds]
+    off = [j for j in dests if topo.chip(cores[j]) != chip]
+    on = [j for j in dests if topo.chip(cores[j]) == chip]
+    out = []
+    for group, first_engine in ((off, 0), (on, 8)):
+        if group:
+            width = 8 // len(group)
+            for i, j in enumerate(group):
+                out.append((j, ((1 << width) - 1) << (first_engine + i * width)))
+    return cores.index(owner), (min(dests) // HALF) * HALF, out
+
+
+def engines(mask):
+    return bin(mask).count("1")
+
+
+def dst_id(topo, c):
+    rid, pid, _sengine = topo.addr(c)
+    return DstId(rid=rid, pnc=pid)
+
 
 def rank_program(g, core, T, topo):
-    r = T.rank_of(core)
-    if r is None:
+    cores = list(T.cores)
+    chip = topo.chip(core)
+    r, base, writes = column_writes(core, cores, topo)
+    is_rank = T.rank_of(core) is not None
+    left = sum(engines(m) for _j, m in writes)
+
+    if is_rank:
+        g.sync.dma_start(T.xs[:], T.x[:]).then_inc(T.sem.loaded, 16)
+        g.wait_ge(T.sem.loaded, 16)
+        by_half = {}
+        for local in ROLES[core % 8]:
+            helper = chip * 8 + local
+            if helper != core:
+                by_half.setdefault(column_writes(helper, cores, topo)[1], []).append(helper)
+        feed = []
+        for i, lo in enumerate(sorted(by_half, key=lambda h: len(by_half[h]))):
+            helpers = by_half[lo]
+            feed.append(RemoteDMATransfer(
+                dst_ids=[dst_id(topo, h) for h in helpers], dma_engine_mask=0xFF << (8 * i),
+                remote_sem=T.sem.arrived, srcs=[T.xs[:, lo:lo + HALF]], dsts=[T.half[:] for _h in helpers]))
+        g.remote_dma_fused(feed, local_sem=T.sem.arrived)
+        left += FEED_ENGINES * len(feed)
+        src, base = T.xs, 0
+    else:
+        g.wait_ge(T.sem.arrived, FEED_ENGINES)
+        left += FEED_ENGINES
+        src = T.half
+
+    g.remote_dma_fused(
+        [RemoteDMATransfer(dst_ids=[dst_id(topo, cores[j])], dma_engine_mask=m, remote_sem=T.sem.arrived,
+                           src=src[:, j - base:j - base + 1], dst=T.land[:, r:r + 1]) for j, m in writes],
+        local_sem=T.sem.arrived)
+
+    if not is_rank:
+        g.wait_ge(T.sem.arrived, left)
         return
-    n = len(T.cores)
 
-    g.sync.dma_start(T.xs[:], T.x[:]).then_inc(T.sem.loaded, 16)
-
-    g.sync.wait_ge(T.sem.loaded, 16)
-    g.sync.dma_start(T.land[:, r:r + 1], T.xs[:, r:r + 1]).then_inc(T.sem.arrived, 16)
-
-    g.wait_ge(T.sem.loaded, 16)
-    off = [j for j in range(n) if topo.chip(T.cores[j]) != topo.chip(core)]
-    on = [j for j in range(n) if j != r and topo.chip(T.cores[j]) == topo.chip(core)]
-
-    def transfer(j, engine):
-        rid, pid, _se = topo.addr(T.cores[j])
-        return RemoteDMATransfer(dst_ids=[DstId(rid=rid, pnc=pid)], dma_engine_mask=1 << engine,
-                                 remote_sem=T.sem.arrived, src=T.xs[:, j:j + 1], dst=T.land[:, r:r + 1])
-
-    half = len(off) // 2
-    first = [transfer(j, e) for e, j in enumerate(off[:half])] + [transfer(j, 8 + e) for e, j in enumerate(on)]
-    second = [transfer(j, e) for e, j in enumerate(off[half:])]
-    g.remote_dma_fused(first, local_sem=T.sem.arrived)
-    g.remote_dma_fused(second, local_sem=T.sem.arrived)
-
-    g.wait_ge(T.sem.arrived, 16 + 2 * (n - 1))
-    g.dma_start(T.y[:], T.land[:]).then_inc(T.sem.stored, 16)
-    g.wait_ge(T.sem.stored, 16)
+    me = T.rank_of(core)
+    landed = 0
+    for c in cores:
+        for local in ROLES[c % 8]:
+            landed += sum(engines(m) for j, m in column_writes(topo.chip(c) * 8 + local, cores, topo)[2] if j == me)
+    g.sync.wait_ge(T.sem.arrived, left + landed)
+    g.sync.dma_start(T.y[:], T.land[:]).then_inc(T.sem.stored, 16)
+    g.sync.wait_ge(T.sem.stored, 16)

from concourse.bass import DstId, RemoteDMATransfer

HALF = 8

SCRATCH = {
    "xs": ("sbuf", [128, 16], "bfloat16"),
    "half": ("sbuf", [128, HALF], "bfloat16"),
    "land": ("sbuf", [128, 16], "bfloat16"),
}
SEMAPHORES = ["loaded", "arrived", "stored"]

ROLES = {
    2: {2: (1, 3), 0: (0, 2), 4: (4, 6), 6: (5, 7)},
    3: {3: (5, 7), 1: (4, 6), 5: (0, 2), 7: (1, 3)},
}
FEED_ENGINES = 8


def column_writes(sender, cores, topo):
    chip, local = topo.chip(sender), sender % 8
    owner = [c for c in cores if topo.chip(c) == chip and local in ROLES[c % 8]][0]
    ds = ROLES[owner % 8][local]
    dests = [j for j, c in enumerate(cores) if (topo.chip(c) ^ chip) in ds]
    off = [j for j in dests if topo.chip(cores[j]) != chip]
    on = [j for j in dests if topo.chip(cores[j]) == chip]
    out = []
    for group, first_engine in ((off, 0), (on, 8)):
        if group:
            width = 8 // len(group)
            for i, j in enumerate(group):
                out.append((j, ((1 << width) - 1) << (first_engine + i * width)))
    return cores.index(owner), (min(dests) // HALF) * HALF, out


def engines(mask):
    return bin(mask).count("1")


def dst_id(topo, c):
    rid, pid, _sengine = topo.addr(c)
    return DstId(rid=rid, pnc=pid)


def rank_program(g, core, T, topo):
    cores = list(T.cores)
    chip = topo.chip(core)
    r, base, writes = column_writes(core, cores, topo)
    is_rank = T.rank_of(core) is not None
    left = sum(engines(m) for _j, m in writes)

    if is_rank:
        g.sync.dma_start(T.xs[:], T.x[:]).then_inc(T.sem.loaded, 16)
        g.wait_ge(T.sem.loaded, 16)
        by_half = {}
        for local in ROLES[core % 8]:
            helper = chip * 8 + local
            if helper != core:
                by_half.setdefault(column_writes(helper, cores, topo)[1], []).append(helper)
        feed = []
        for i, lo in enumerate(sorted(by_half, key=lambda h: len(by_half[h]))):
            helpers = by_half[lo]
            feed.append(RemoteDMATransfer(
                dst_ids=[dst_id(topo, h) for h in helpers], dma_engine_mask=0xFF << (8 * i),
                remote_sem=T.sem.arrived, srcs=[T.xs[:, lo:lo + HALF]], dsts=[T.half[:] for _h in helpers]))
        g.remote_dma_fused(feed, local_sem=T.sem.arrived)
        left += FEED_ENGINES * len(feed)
        src, base = T.xs, 0
    else:
        g.wait_ge(T.sem.arrived, FEED_ENGINES)
        left += FEED_ENGINES
        src = T.half

    g.remote_dma_fused(
        [RemoteDMATransfer(dst_ids=[dst_id(topo, cores[j])], dma_engine_mask=m, remote_sem=T.sem.arrived,
                           src=src[:, j - base:j - base + 1], dst=T.land[:, r:r + 1]) for j, m in writes],
        local_sem=T.sem.arrived)

    if not is_rank:
        g.wait_ge(T.sem.arrived, left)
        return

    me = T.rank_of(core)
    landed = 0
    for c in cores:
        for local in ROLES[c % 8]:
            landed += sum(engines(m) for j, m in column_writes(topo.chip(c) * 8 + local, cores, topo)[2] if j == me)
    g.sync.wait_ge(T.sem.arrived, left + landed)
    g.sync.dma_start(T.y[:], T.land[:]).then_inc(T.sem.stored, 16)
    g.sync.wait_ge(T.sem.stored, 16)
